import numpy as np
import ml_dtypes


def mxq(x, axis, fmt="e4m3"):
    dtype, down = {"e4m3": (ml_dtypes.float8_e4m3fn, 7), "e5m2": (ml_dtypes.float8_e5m2, 14)}[fmt]
    v = np.moveaxis(np.asarray(x, np.float32).astype(ml_dtypes.bfloat16).astype(np.float64), axis, -1)
    blocks = v.reshape(v.shape[:-1] + (-1, 32))
    amax = np.abs(blocks).max(-1, keepdims=True)
    byte = np.maximum(np.where(amax > 0, np.frexp(amax)[1] - 1 + 127, 0) - down, 1)
    scale = np.exp2(byte - 127.0)
    codes = (blocks / scale).astype(np.float32).astype(dtype).astype(np.float64)
    return np.moveaxis((codes * scale).reshape(v.shape), -1, axis)


WIDE = False


def mx_kscale(k):
    if not WIDE:
        return np.ones(k)
    levels = np.array([10, -10, 5, -5, 0])
    if k % 512:
        return np.exp2(np.random.permutation(np.resize(levels, k // 32))).repeat(32)
    a = np.empty((k // 512, 16))
    for p in range(k // 512):
        a[p, :8] = np.random.permutation(np.resize(levels, 8))
        for g in range(8):
            far = levels[np.abs(levels - a[p, g]) >= 10]
            a[p, g + 8] = far[np.random.randint(len(far))]
    return np.exp2(a.ravel()).repeat(32)


def f64(x):
    return np.asarray(x).astype(np.float64)


def striped(idx):
    return np.tile(np.asarray(idx).reshape(-1, 16).T, (8, 1)).astype(np.uint16)


def unstriped(offs):
    return offs[:16].T.reshape(-1).astype(np.int64)


B, N, T, D, DV, NQ = 1, 512, 2048, 512, 256, 256


def setup_inputs():
    n = np.random.standard_normal
    idx = np.sort(np.random.permutation(T)[:B * N].reshape(B, N), axis=1).reshape(-1)
    s = mx_kscale(D)[:, None]
    u = np.ones(T)
    u[idx] = mx_kscale(B * N)
    r = np.random.uniform(0.5, 2.0, T)
    rk = np.random.uniform(0.5, 2.0, T)
    k = n((D, T)) / s / rk
    v = n((DV, T)) / (u * r)
    return {
        "qT": (n((B, D, NQ)) * s * (0.50 / np.sqrt(D))).astype(np.float32),
        "kT": k.astype(np.float32),
        "vT": v.astype(np.float32),
        "ks": np.tile(rk, (128, 1)).astype(np.float32),
        "vs": np.tile(u * r, (128, 1)).astype(np.float32),
        "og": n((B, NQ, DV)).astype(np.float32),
        "offs": striped(idx),
    }


def reference(qT, kT, vT, ks, vs, og, offs):
    idx = unstriped(offs)
    k = f64(kT)
    v = f64(vT)
    pick = lambda x: x[:, idx].reshape(x.shape[0], B, N).transpose(1, 0, 2)
    q = f64(qT)
    score = mxq(q, 1, "e4m3").transpose(0, 2, 1) @ mxq(pick(k), 1, "e4m3")
    score = score * pick(f64(ks))[:, :1, :]
    m = score.max(-1, keepdims=True)
    p = np.exp(score - m)
    total = p.sum(-1, keepdims=True)
    w = p * pick(f64(vs))[:, :1, :]
    y = mxq(w, 2, "e4m3") @ mxq(pick(v).transpose(0, 2, 1), 1, "e4m3")
    y = y / total
    y = y / (1.0 + np.exp(-f64(og)))
    return y

@@ -1,0 +1,198 @@
+from contextlib import ExitStack
+
+import concourse.mybir as mybir
+from concourse.masks import make_identity
+
+P = 128
+D, NQ, T, N, DV = 512, 256, 2048, 512, 256
+PACK = 4
+S = N // PACK
+
+FLOPS = 2 * NQ * N * D + 2 * NQ * N * DV
+BYTES = 4 * (D * NQ + D * T + DV * T + 2 * T + 2 * NQ * DV) + 2 * P * (N // 16)
+
+F32 = mybir.dt.float32
+BF16 = mybir.dt.bfloat16
+U16 = mybir.dt.uint16
+U32 = mybir.dt.uint32
+U8 = mybir.dt.uint8
+FP8X4 = mybir.dt.float8_e4m3fn_x4
+
+ACT = mybir.ActivationFunctionType
+ALU = mybir.AluOpType
+AX = mybir.AxisListType
+
+
+def tile_attend_gate_topks_kernel(tc, qT, kT, vT, ks, vs, og, offs, out):
+    nc = tc.nc
+    with ExitStack() as ctx:
+        keep = ctx.enter_context(tc.tile_pool(name="keep", bufs=1))
+        psum = ctx.enter_context(tc.psum_pool(name="psum", bufs=2))
+
+        offsets = keep.tile([P, N // 16], U16, name="offsets")
+        nc.sync.dma_start(offsets[:], offs)
+
+        scale_win = []
+        for i, engine in enumerate((nc.vector, nc.gpsimd)):
+            win = keep.tile([P, T], F32, name=f"scale_win{i}")
+            engine.memset(win[:], 0.0)
+            scale_win.append(win)
+
+        q_raw = keep.tile([P, PACK, NQ], F32, name="q_raw")
+        nc.sync.dma_start(out=q_raw[:], in_=qT.rearrange("o (p t) q -> p (o t) q", t=PACK))
+        k_rows = kT.rearrange("(p t) n -> p t n", t=PACK)
+        k_raw = []
+        for t in range(PACK):
+            plane = keep.tile([P, T], F32, name=f"k_raw{t}")
+            nc.sync.dma_start(out=plane[:], in_=k_rows[:, t, :])
+            k_raw.append(plane)
+            if t == 0:
+                for win, src in zip(scale_win, (ks, vs)):
+                    nc.sync.dma_start(out=win[0:1, :], in_=src[0:1, :])
+        v_raw = []
+        for e in range(DV // P):
+            block = keep.tile([P, T], F32, name=f"v_raw{e}")
+            nc.sync.dma_start(out=block[:], in_=vT[e * P : (e + 1) * P, :])
+            v_raw.append(block)
+        og_raw = keep.tile([P, 2, DV], F32, name="og_raw")
+        nc.sync.dma_start(out=og_raw[:], in_=og.rearrange("o (b p) e -> p (o b) e", p=P))
+
+        warm = keep.tile([P, 1], F32, name="warm")
+        nc.vector.memset(warm[:], 0.0)
+        warmed = keep.tile([P, 1], F32, name="warmed")
+        nc.scalar.activation(warmed[:], warm[:], ACT.Exp)
+
+        ident = keep.tile([P, P], F32, name="ident")
+        ident_bf = keep.tile([P, P], BF16, name="ident_bf")
+
+        make_identity(nc, ident[:])
+        make_identity(nc, ident_bf[:])
+
+        q_bf = keep.tile([P, NQ, PACK], BF16, name="q_bf", align_bytes=64)
+        nc.scalar.copy(q_bf[:], q_raw[:].rearrange("p t q -> p q t"))
+        q_codes = keep.tile([P, NQ], U32, name="q_codes", align_bytes=64)
+        q_scales = keep.tile([P, NQ], U8, name="q_scales", align_bytes=64)
+        nc.vector.quantize_mx(out=q_codes[:].bitcast(FP8X4), scales=q_scales[:], in_=q_bf[:].rearrange("p q t -> p (q t)"))
+
+        scale_cols = []
+        for i in range(2):
+            picked = keep.tile([P, N], F32, name=f"scale_row{i}")
+            nc.vector.tensor_copy(picked[:], scale_win[i][:].indirect(offsets[:]))
+            turned = psum.tile([P, PACK, P], F32, tag="a", name=f"scale_turned{i}")
+            for a in range(PACK):
+                nc.tensor.transpose(turned[:, a, :], picked[:, a::PACK], ident[:])
+            cols = keep.tile([P, PACK], F32, name=f"scale_cols{i}")
+            nc.scalar.copy(cols[:], turned[:, :, 0])
+            scale_cols.append(cols)
+        ks_cols, vs_cols = scale_cols
+
+        k_bf = keep.tile([P, PACK, S, PACK], BF16, name="k_bf", align_bytes=64)
+        for t in range(PACK):
+            nc.vector.tensor_copy(k_bf[:, :, :, t].rearrange("p a s -> p s a"), k_raw[t][:].indirect(offsets[:]))
+        k_codes = keep.tile([P, N], U32, name="k_codes", align_bytes=64)
+        k_scales = keep.tile([P, N], U8, name="k_scales", align_bytes=64)
+        scaled = keep.tile([P, PACK, NQ], F32, name="scaled")
+        for h in range(2):
+            cols = slice(h * 2 * S, (h + 1) * 2 * S)
+            nc.vector.quantize_mx(
+                out=k_codes[:, cols].bitcast(FP8X4),
+                scales=k_scales[:, cols],
+                in_=k_bf[:, 2 * h : 2 * h + 2, :, :].rearrange("p a s t -> p (a s t)"),
+            )
+        for h in range(2):
+            scores = psum.tile([P, 2, NQ], F32, tag="s", name=f"scores{h}")
+            for i in range(2):
+                a = 2 * h + i
+                nc.tensor.matmul_mx(
+                    out=scores[:, i, :],
+                    lhsT=k_codes[:, a * S : (a + 1) * S].bitcast(FP8X4),
+                    lhsT_scale=k_scales[:, a * S : (a + 1) * S],
+                    rhs=q_codes[:].bitcast(FP8X4),
+                    rhs_scale=q_scales[:],
+                    start=True,
+                    stop=True,
+                )
+                if h == 0:
+                    nc.scalar.activation(scaled[:, a, :], scores[:, i, :], ACT.Copy, scale=ks_cols[:, a : a + 1])
+                else:
+                    nc.vector.tensor_scalar(scaled[:, a, :], scores[:, i, :], ks_cols[:, a : a + 1], None, op0=ALU.mult)
+
+        neg_max = []
+        sums = keep.tile([P, 2], F32, name="sums")
+        probs = []
+        for b in range(2):
+            rows = psum.tile([P, PACK, S], F32, tag="a", name=f"rows{b}")
+            for a in range(PACK):
+                nc.tensor.transpose(rows[:, a, :], scaled[:, a, b * P : (b + 1) * P], ident[:])
+            top = keep.tile([P, 1], F32, name=f"top{b}")
+            nc.vector.reduce_max(out=top[:], in_=rows[:].rearrange("p a s -> p (a s)"), axis=AX.X, negate=True)
+            prob = keep.tile([P, PACK, S], F32, name=f"prob{b}")
+            nc.scalar.activation(prob[:], rows[:], ACT.Exp, bias=top[:], accum_out=sums[:, b : b + 1])
+            probs.append(prob)
+
+        v_codes, v_scales = [], []
+
+        def pick_values(e):
+            v_bf = keep.tile([P, PACK, S], BF16, name=f"v_bf{e}", align_bytes=64)
+            nc.vector.tensor_copy(v_bf[:].rearrange("p a s -> p s a"), v_raw[e][:].indirect(offsets[:]))
+            turned = psum.tile([P, PACK, P], BF16, tag="v", name=f"v_turned{e}")
+            for a in range(PACK):
+                nc.tensor.transpose(turned[:, a, :], v_bf[:, a, :], ident_bf[:])
+            grouped = keep.tile([P, P, PACK], BF16, name=f"v_grouped{e}", align_bytes=64)
+            nc.scalar.copy(grouped[:], turned[:].rearrange("p a e -> p e a"))
+            codes = keep.tile([P, P], U32, name=f"v_codes{e}", align_bytes=64)
+            scales = keep.tile([P, P], U8, name=f"v_scales{e}", align_bytes=64)
+            nc.vector.quantize_mx(out=codes[:].bitcast(FP8X4), scales=scales[:], in_=grouped[:].rearrange("p e a -> p (e a)"))
+            v_codes.append(codes)
+            v_scales.append(scales)
+
+        pick_values(0)
+
+        w_codes, w_scales = [], []
+        for b in range(2):
+            turned = psum.tile([P, PACK, P], F32, tag="s", name=f"p_turned{b}")
+            for a in range(PACK):
+                nc.tensor.transpose(turned[:, a, :], probs[b][:, a, :], ident[:])
+            w_bf = keep.tile([P, P, PACK], BF16, name=f"w_bf{b}", align_bytes=64)
+            nc.vector.tensor_tensor(
+                w_bf[:],
+                turned[:].rearrange("p a q -> p q a"),
+                vs_cols[:].unsqueeze(1).to_broadcast([P, P, PACK]),
+                ALU.mult,
+            )
+            codes = keep.tile([P, P], U32, name=f"w_codes{b}", align_bytes=64)
+            scales = keep.tile([P, P], U8, name=f"w_scales{b}", align_bytes=64)
+            nc.vector.quantize_mx(out=codes[:].bitcast(FP8X4), scales=scales[:], in_=w_bf[:].rearrange("p q a -> p (q a)"))
+            w_codes.append(codes)
+            w_scales.append(scales)
+
+        pick_values(1)
+
+        inv = keep.tile([P, 2], F32, name="inv")
+        nc.vector.reciprocal(inv[:], sums[:])
+        half_inv = keep.tile([P, 2], F32, name="half_inv")
+        nc.gpsimd.tensor_scalar(half_inv[:], inv[:], 0.5, None, op0=ALU.mult)
+        gate = keep.tile([P, 2, DV], F32, name="gate")
+        nc.scalar.activation(gate[:], og_raw[:], ACT.Tanh, scale=0.5)
+        factor = keep.tile([P, 2, DV], F32, name="factor")
+        for b in range(2):
+            nc.scalar.activation(
+                factor[:, b, :], gate[:, b, :], ACT.Identity, scale=half_inv[:, b : b + 1], bias=half_inv[:, b : b + 1]
+            )
+
+        out_rows = out.rearrange("o (b p) e -> p (o b) e", p=P)
+        for e in range(2):
+            y = psum.tile([P, 2, P], F32, tag="y", name=f"y{e}")
+            for b in range(2):
+                nc.tensor.matmul_mx(
+                    out=y[:, b, :],
+                    lhsT=w_codes[b][:].bitcast(FP8X4),
+                    lhsT_scale=w_scales[b][:],
+                    rhs=v_codes[e][:].bitcast(FP8X4),
+                    rhs_scale=v_scales[e][:],
+                    start=True,
+                    stop=True,
+                )
+            result = keep.tile([P, 2, P], F32, name=f"result{e}")
+            nc.vector.tensor_tensor(result[:], y[:], factor[:, :, e * P : (e + 1) * P], ALU.mult)
+            nc.sync.dma_start(out=out_rows[:, :, e * P : (e + 1) * P], in_=result[:])

@@ -38,8 +38,6 @@ def tile_attend_gate_topks_kernel(tc, qT, kT, vT, ks, vs, og, offs, out):
             engine.memset(win[:], 0.0)
             scale_win.append(win)
 
-        q_raw = keep.tile([P, PACK, NQ], F32, name="q_raw")
-        nc.sync.dma_start(out=q_raw[:], in_=qT.rearrange("o (p t) q -> p (o t) q", t=PACK))
         k_rows = kT.rearrange("(p t) n -> p t n", t=PACK)
         k_raw = []
         for t in range(PACK):
@@ -49,6 +47,8 @@ def tile_attend_gate_topks_kernel(tc, qT, kT, vT, ks, vs, og, offs, out):
             if t == 0:
                 for win, src in zip(scale_win, (ks, vs)):
                     nc.sync.dma_start(out=win[0:1, :], in_=src[0:1, :])
+        q_raw = keep.tile([P, PACK, NQ], F32, name="q_raw")
+        nc.sync.dma_start(out=q_raw[:], in_=qT.rearrange("o (p t) q -> p (o t) q", t=PACK))
         v_raw = []
         for e in range(DV // P):
             block = keep.tile([P, T], F32, name=f"v_raw{e}")
@@ -68,27 +68,25 @@ def tile_attend_gate_topks_kernel(tc, qT, kT, vT, ks, vs, og, offs, out):
         make_identity(nc, ident[:])
         make_identity(nc, ident_bf[:])
 
-        q_bf = keep.tile([P, NQ, PACK], BF16, name="q_bf", align_bytes=64)
-        nc.scalar.copy(q_bf[:], q_raw[:].rearrange("p t q -> p q t"))
-        q_codes = keep.tile([P, NQ], U32, name="q_codes", align_bytes=64)
-        q_scales = keep.tile([P, NQ], U8, name="q_scales", align_bytes=64)
-        nc.vector.quantize_mx(out=q_codes[:].bitcast(FP8X4), scales=q_scales[:], in_=q_bf[:].rearrange("p q t -> p (q t)"))
-
         scale_cols = []
         for i in range(2):
             picked = keep.tile([P, N], F32, name=f"scale_row{i}")
             nc.vector.tensor_copy(picked[:], scale_win[i][:].indirect(offsets[:]))
             turned = psum.tile([P, PACK, P], F32, tag="a", name=f"scale_turned{i}")
             for a in range(PACK):
-                nc.tensor.transpose(turned[:, a, :], picked[:, a::PACK], ident[:])
+                nc.tensor.transpose(turned[:, a, :], picked[:, a * S : (a + 1) * S] if i == 0 else picked[:, a::PACK], ident[:])
             cols = keep.tile([P, PACK], F32, name=f"scale_cols{i}")
             nc.scalar.copy(cols[:], turned[:, :, 0])
             scale_cols.append(cols)
         ks_cols, vs_cols = scale_cols
 
-        k_bf = keep.tile([P, PACK, S, PACK], BF16, name="k_bf", align_bytes=64)
-        for t in range(PACK):
-            nc.vector.tensor_copy(k_bf[:, :, :, t].rearrange("p a s -> p s a"), k_raw[t][:].indirect(offsets[:]))
+        k_bf = keep.tile([P, N, PACK], BF16, name="k_bf", align_bytes=64)
+        for t in range(PACK - 1):
+            nc.vector.tensor_copy(k_bf[:, :, t], k_raw[t][:].indirect(offsets[:]))
+        for h in range(2):
+            nc.vector.tensor_copy(
+                k_bf[:, h * 2 * S : (h + 1) * 2 * S, PACK - 1], k_raw[PACK - 1][:].indirect(offsets[:, h * 16 : (h + 1) * 16])
+            )
         k_codes = keep.tile([P, N], U32, name="k_codes", align_bytes=64)
         k_scales = keep.tile([P, N], U8, name="k_scales", align_bytes=64)
         scaled = keep.tile([P, PACK, NQ], F32, name="scaled")
@@ -97,14 +95,19 @@ def tile_attend_gate_topks_kernel(tc, qT, kT, vT, ks, vs, og, offs, out):
             nc.vector.quantize_mx(
                 out=k_codes[:, cols].bitcast(FP8X4),
                 scales=k_scales[:, cols],
-                in_=k_bf[:, 2 * h : 2 * h + 2, :, :].rearrange("p a s t -> p (a s t)"),
+                in_=k_bf[:, cols, :].rearrange("p s t -> p (s t)"),
             )
-        for h in range(2):
-            scores = psum.tile([P, 2, NQ], F32, tag="s", name=f"scores{h}")
-            for i in range(2):
-                a = 2 * h + i
+        for b in range(2):
+            queries = slice(b * P, (b + 1) * P)
+            q_bf = keep.tile([P, P, PACK], BF16, name=f"q_bf{b}", align_bytes=64)
+            nc.scalar.copy(q_bf[:], q_raw[:, :, queries].rearrange("p t q -> p q t"))
+            q_codes = keep.tile([P, P], U32, name=f"q_codes{b}", align_bytes=64)
+            q_scales = keep.tile([P, P], U8, name=f"q_scales{b}", align_bytes=64)
+            nc.vector.quantize_mx(out=q_codes[:].bitcast(FP8X4), scales=q_scales[:], in_=q_bf[:].rearrange("p q t -> p (q t)"))
+            scores = psum.tile([P, PACK, P], F32, tag="s", name=f"scores{b}")
+            for a in range(PACK):
                 nc.tensor.matmul_mx(
-                    out=scores[:, i, :],
+                    out=scores[:, a, :],
                     lhsT=k_codes[:, a * S : (a + 1) * S].bitcast(FP8X4),
                     lhsT_scale=k_scales[:, a * S : (a + 1) * S],
                     rhs=q_codes[:].bitcast(FP8X4),
@@ -112,13 +115,14 @@ def tile_attend_gate_topks_kernel(tc, qT, kT, vT, ks, vs, og, offs, out):
                     start=True,
                     stop=True,
                 )
-                if h == 0:
-                    nc.scalar.activation(scaled[:, a, :], scores[:, i, :], ACT.Copy, scale=ks_cols[:, a : a + 1])
-                else:
-                    nc.vector.tensor_scalar(scaled[:, a, :], scores[:, i, :], ks_cols[:, a : a + 1], None, op0=ALU.mult)
+            for a in range(PACK):
+                if b == 0 and a == 2:
+                    nc.vector.tensor_tensor(scaled[:, 2:, queries], scores[:, 2:, :], ks_cols[:, 2:].unsqueeze(2).to_broadcast([P, 2, P]), ALU.mult)
+                elif b == 1 or a < 2:
+                    nc.scalar.activation(scaled[:, a, queries], scores[:, a, :], ACT.Copy, scale=ks_cols[:, a : a + 1])
 
         neg_max = []
-        sums = keep.tile([P, 2], F32, name="sums")
+        parts = [keep.tile([P, 2], F32, name=f"parts{h}") for h in range(2)]
         probs = []
         for b in range(2):
             rows = psum.tile([P, PACK, S], F32, tag="a", name=f"rows{b}")
@@ -127,8 +131,21 @@ def tile_attend_gate_topks_kernel(tc, qT, kT, vT, ks, vs, og, offs, out):
             top = keep.tile([P, 1], F32, name=f"top{b}")
             nc.vector.reduce_max(out=top[:], in_=rows[:].rearrange("p a s -> p (a s)"), axis=AX.X, negate=True)
             prob = keep.tile([P, PACK, S], F32, name=f"prob{b}")
-            nc.scalar.activation(prob[:], rows[:], ACT.Exp, bias=top[:], accum_out=sums[:, b : b + 1])
+            by_class = rows[:].rearrange("p n (s a) -> p a n s", a=PACK)
+            for h in range(2):
+                nc.scalar.activation(
+                    prob[:, 2 * h : 2 * h + 2, :].rearrange("p a (n s) -> p a n s", n=PACK),
+                    by_class[:, 2 * h : 2 * h + 2, :, :],
+                    ACT.Exp,
+                    bias=top[:],
+                    accum_out=parts[h][:, b : b + 1],
+                )
             probs.append(prob)
+
+        sums = keep.tile([P, 2], F32, name="sums")
+        nc.vector.tensor_tensor(sums[:], parts[0][:], parts[1][:], ALU.add)
+        inv = keep.tile([P, 2], F32, name="inv")
+        nc.vector.reciprocal(inv[:], sums[:])
 
         v_codes, v_scales = [], []
 
@@ -147,6 +164,10 @@ def tile_attend_gate_topks_kernel(tc, qT, kT, vT, ks, vs, og, offs, out):
             v_scales.append(scales)
 
         pick_values(0)
+
+        gate = keep.tile([P, 2, DV], F32, name="gate")
+        nc.scalar.activation(gate[:], og_raw[:], ACT.Tanh, scale=0.5)
+        factor = keep.tile([P, 2, DV], F32, name="factor")
 
         w_codes, w_scales = [], []
         for b in range(2):
@@ -168,16 +189,9 @@ def tile_attend_gate_topks_kernel(tc, qT, kT, vT, ks, vs, og, offs, out):
 
         pick_values(1)
 
-        inv = keep.tile([P, 2], F32, name="inv")
-        nc.vector.reciprocal(inv[:], sums[:])
-        half_inv = keep.tile([P, 2], F32, name="half_inv")
-        nc.gpsimd.tensor_scalar(half_inv[:], inv[:], 0.5, None, op0=ALU.mult)
-        gate = keep.tile([P, 2, DV], F32, name="gate")
-        nc.scalar.activation(gate[:], og_raw[:], ACT.Tanh, scale=0.5)
-        factor = keep.tile([P, 2, DV], F32, name="factor")
         for b in range(2):
             nc.scalar.activation(
-                factor[:, b, :], gate[:, b, :], ACT.Identity, scale=half_inv[:, b : b + 1], bias=half_inv[:, b : b + 1]
+                factor[:, b, :], gate[:, b, :], ACT.Identity, scale=inv[:, b : b + 1], bias=inv[:, b : b + 1]
             )
 
         out_rows = out.rearrange("o (b p) e -> p (o b) e", p=P)
@@ -194,5 +208,5 @@ def tile_attend_gate_topks_kernel(tc, qT, kT, vT, ks, vs, og, offs, out):
                     stop=True,
                 )
             result = keep.tile([P, 2, P], F32, name=f"result{e}")
-            nc.vector.tensor_tensor(result[:], y[:], factor[:, :, e * P : (e + 1) * P], ALU.mult)
+            nc.vector.scalar_tensor_tensor(result[:], y[:], 0.5, factor[:, :, e * P : (e + 1) * P], ALU.mult, ALU.mult)
             nc.sync.dma_start(out=out_rows[:, :, e * P : (e + 1) * P], in_=result[:])

@@ -33,9 +33,9 @@ def tile_attend_gate_topks_kernel(tc, qT, kT, vT, ks, vs, og, offs, out):
         nc.sync.dma_start(offsets[:], offs)
 
         scale_win = []
-        for i, engine in enumerate((nc.vector, nc.gpsimd)):
+        for i in range(2):
             win = keep.tile([P, T], F32, name=f"scale_win{i}")
-            engine.memset(win[:], 0.0)
+            nc.vector.memset(win[:], 0.0)
             scale_win.append(win)
 
         k_rows = kT.rearrange("(p t) n -> p t n", t=PACK)
@@ -44,9 +44,8 @@ def tile_attend_gate_topks_kernel(tc, qT, kT, vT, ks, vs, og, offs, out):
             plane = keep.tile([P, T], F32, name=f"k_raw{t}")
             nc.sync.dma_start(out=plane[:], in_=k_rows[:, t, :])
             k_raw.append(plane)
-            if t == 0:
-                for win, src in zip(scale_win, (ks, vs)):
-                    nc.sync.dma_start(out=win[0:1, :], in_=src[0:1, :])
+            if t < 2:
+                nc.sync.dma_start(out=scale_win[t][0:1, :], in_=(ks, vs)[t][0:1, :])
         q_raw = keep.tile([P, PACK, NQ], F32, name="q_raw")
         nc.sync.dma_start(out=q_raw[:], in_=qT.rearrange("o (p t) q -> p (o t) q", t=PACK))
         v_raw = []

@@ -30,8 +30,6 @@ def tile_attend_gate_topks_kernel(tc, qT, kT, vT, ks, vs, og, offs, out):
         psum = ctx.enter_context(tc.psum_pool(name="psum", bufs=2))
 
         offsets = keep.tile([P, N // 16], U16, name="offsets")
-        nc.sync.dma_start(offsets[:], offs)
-
         scale_win = []
         for i in range(2):
             win = keep.tile([P, T], F32, name=f"scale_win{i}")
@@ -44,6 +42,8 @@ def tile_attend_gate_topks_kernel(tc, qT, kT, vT, ks, vs, og, offs, out):
             plane = keep.tile([P, T], F32, name=f"k_raw{t}")
             nc.sync.dma_start(out=plane[:], in_=k_rows[:, t, :])
             k_raw.append(plane)
+            if t == 0:
+                nc.sync.dma_start(offsets[:], offs)
             if t < 2:
                 nc.sync.dma_start(out=scale_win[t][0:1, :], in_=(ks, vs)[t][0:1, :])
         q_raw = keep.tile([P, PACK, NQ], F32, name="q_raw")
@@ -57,7 +57,7 @@ def tile_attend_gate_topks_kernel(tc, qT, kT, vT, ks, vs, og, offs, out):
         nc.sync.dma_start(out=og_raw[:], in_=og.rearrange("o (b p) e -> p (o b) e", p=P))
 
         warm = keep.tile([P, 1], F32, name="warm")
-        nc.vector.memset(warm[:], 0.0)
+        nc.gpsimd.memset(warm[:], 0.0)
         warmed = keep.tile([P, 1], F32, name="warmed")
         nc.scalar.activation(warmed[:], warm[:], ACT.Exp)
 

from contextlib import ExitStack

import concourse.mybir as mybir
from concourse.masks import make_identity

P = 128
D, NQ, T, N, DV = 512, 256, 2048, 512, 256
PACK = 4
S = N // PACK

FLOPS = 2 * NQ * N * D + 2 * NQ * N * DV
BYTES = 4 * (D * NQ + D * T + DV * T + 2 * T + 2 * NQ * DV) + 2 * P * (N // 16)

F32 = mybir.dt.float32
BF16 = mybir.dt.bfloat16
U16 = mybir.dt.uint16
U32 = mybir.dt.uint32
U8 = mybir.dt.uint8
FP8X4 = mybir.dt.float8_e4m3fn_x4

ACT = mybir.ActivationFunctionType
ALU = mybir.AluOpType
AX = mybir.AxisListType


def tile_attend_gate_topks_kernel(tc, qT, kT, vT, ks, vs, og, offs, out):
    nc = tc.nc
    with ExitStack() as ctx:
        keep = ctx.enter_context(tc.tile_pool(name="keep", bufs=1))
        psum = ctx.enter_context(tc.psum_pool(name="psum", bufs=2))

        offsets = keep.tile([P, N // 16], U16, name="offsets")
        scale_win = []
        for i in range(2):
            win = keep.tile([P, T], F32, name=f"scale_win{i}")
            nc.vector.memset(win[:], 0.0)
            scale_win.append(win)

        k_rows = kT.rearrange("(p t) n -> p t n", t=PACK)
        k_raw = []
        for t in range(PACK):
            plane = keep.tile([P, T], F32, name=f"k_raw{t}")
            nc.sync.dma_start(out=plane[:], in_=k_rows[:, t, :])
            k_raw.append(plane)
            if t == 0:
                nc.sync.dma_start(offsets[:], offs)
            if t < 2:
                nc.sync.dma_start(out=scale_win[t][0:1, :], in_=(ks, vs)[t][0:1, :])
        q_raw = keep.tile([P, PACK, NQ], F32, name="q_raw")
        nc.sync.dma_start(out=q_raw[:], in_=qT.rearrange("o (p t) q -> p (o t) q", t=PACK))
        v_raw = []
        for e in range(DV // P):
            block = keep.tile([P, T], F32, name=f"v_raw{e}")
            nc.sync.dma_start(out=block[:], in_=vT[e * P : (e + 1) * P, :])
            v_raw.append(block)
        og_raw = keep.tile([P, 2, DV], F32, name="og_raw")
        nc.sync.dma_start(out=og_raw[:], in_=og.rearrange("o (b p) e -> p (o b) e", p=P))

        warm = keep.tile([P, 1], F32, name="warm")
        nc.gpsimd.memset(warm[:], 0.0)
        warmed = keep.tile([P, 1], F32, name="warmed")
        nc.scalar.activation(warmed[:], warm[:], ACT.Exp)

        ident = keep.tile([P, P], F32, name="ident")
        ident_bf = keep.tile([P, P], BF16, name="ident_bf")

        make_identity(nc, ident[:])
        make_identity(nc, ident_bf[:])

        scale_cols = []
        for i in range(2):
            picked = keep.tile([P, N], F32, name=f"scale_row{i}")
            nc.vector.tensor_copy(picked[:], scale_win[i][:].indirect(offsets[:]))
            turned = psum.tile([P, PACK, P], F32, tag="a", name=f"scale_turned{i}")
            for a in range(PACK):
                nc.tensor.transpose(turned[:, a, :], picked[:, a * S : (a + 1) * S] if i == 0 else picked[:, a::PACK], ident[:])
            cols = keep.tile([P, PACK], F32, name=f"scale_cols{i}")
            nc.scalar.copy(cols[:], turned[:, :, 0])
            scale_cols.append(cols)
        ks_cols, vs_cols = scale_cols

        k_bf = keep.tile([P, N, PACK], BF16, name="k_bf", align_bytes=64)
        for t in range(PACK - 1):
            nc.vector.tensor_copy(k_bf[:, :, t], k_raw[t][:].indirect(offsets[:]))
        for h in range(2):
            nc.vector.tensor_copy(
                k_bf[:, h * 2 * S : (h + 1) * 2 * S, PACK - 1], k_raw[PACK - 1][:].indirect(offsets[:, h * 16 : (h + 1) * 16])
            )
        k_codes = keep.tile([P, N], U32, name="k_codes", align_bytes=64)
        k_scales = keep.tile([P, N], U8, name="k_scales", align_bytes=64)
        scaled = keep.tile([P, PACK, NQ], F32, name="scaled")
        for h in range(2):
            cols = slice(h * 2 * S, (h + 1) * 2 * S)
            nc.vector.quantize_mx(
                out=k_codes[:, cols].bitcast(FP8X4),
                scales=k_scales[:, cols],
                in_=k_bf[:, cols, :].rearrange("p s t -> p (s t)"),
            )
        for b in range(2):
            queries = slice(b * P, (b + 1) * P)
            q_bf = keep.tile([P, P, PACK], BF16, name=f"q_bf{b}", align_bytes=64)
            nc.scalar.copy(q_bf[:], q_raw[:, :, queries].rearrange("p t q -> p q t"))
            q_codes = keep.tile([P, P], U32, name=f"q_codes{b}", align_bytes=64)
            q_scales = keep.tile([P, P], U8, name=f"q_scales{b}", align_bytes=64)
            nc.vector.quantize_mx(out=q_codes[:].bitcast(FP8X4), scales=q_scales[:], in_=q_bf[:].rearrange("p q t -> p (q t)"))
            scores = psum.tile([P, PACK, P], F32, tag="s", name=f"scores{b}")
            for a in range(PACK):
                nc.tensor.matmul_mx(
                    out=scores[:, a, :],
                    lhsT=k_codes[:, a * S : (a + 1) * S].bitcast(FP8X4),
                    lhsT_scale=k_scales[:, a * S : (a + 1) * S],
                    rhs=q_codes[:].bitcast(FP8X4),
                    rhs_scale=q_scales[:],
                    start=True,
                    stop=True,
                )
            for a in range(PACK):
                if b == 0 and a == 2:
                    nc.vector.tensor_tensor(scaled[:, 2:, queries], scores[:, 2:, :], ks_cols[:, 2:].unsqueeze(2).to_broadcast([P, 2, P]), ALU.mult)
                elif b == 1 or a < 2:
                    nc.scalar.activation(scaled[:, a, queries], scores[:, a, :], ACT.Copy, scale=ks_cols[:, a : a + 1])

        neg_max = []
        parts = [keep.tile([P, 2], F32, name=f"parts{h}") for h in range(2)]
        probs = []
        for b in range(2):
            rows = psum.tile([P, PACK, S], F32, tag="a", name=f"rows{b}")
            for a in range(PACK):
                nc.tensor.transpose(rows[:, a, :], scaled[:, a, b * P : (b + 1) * P], ident[:])
            top = keep.tile([P, 1], F32, name=f"top{b}")
            nc.vector.reduce_max(out=top[:], in_=rows[:].rearrange("p a s -> p (a s)"), axis=AX.X, negate=True)
            prob = keep.tile([P, PACK, S], F32, name=f"prob{b}")
            by_class = rows[:].rearrange("p n (s a) -> p a n s", a=PACK)
            for h in range(2):
                nc.scalar.activation(
                    prob[:, 2 * h : 2 * h + 2, :].rearrange("p a (n s) -> p a n s", n=PACK),
                    by_class[:, 2 * h : 2 * h + 2, :, :],
                    ACT.Exp,
                    bias=top[:],
                    accum_out=parts[h][:, b : b + 1],
                )
            probs.append(prob)

        sums = keep.tile([P, 2], F32, name="sums")
        nc.vector.tensor_tensor(sums[:], parts[0][:], parts[1][:], ALU.add)
        inv = keep.tile([P, 2], F32, name="inv")
        nc.vector.reciprocal(inv[:], sums[:])

        v_codes, v_scales = [], []

        def pick_values(e):
            v_bf = keep.tile([P, PACK, S], BF16, name=f"v_bf{e}", align_bytes=64)
            nc.vector.tensor_copy(v_bf[:].rearrange("p a s -> p s a"), v_raw[e][:].indirect(offsets[:]))
            turned = psum.tile([P, PACK, P], BF16, tag="v", name=f"v_turned{e}")
            for a in range(PACK):
                nc.tensor.transpose(turned[:, a, :], v_bf[:, a, :], ident_bf[:])
            grouped = keep.tile([P, P, PACK], BF16, name=f"v_grouped{e}", align_bytes=64)
            nc.scalar.copy(grouped[:], turned[:].rearrange("p a e -> p e a"))
            codes = keep.tile([P, P], U32, name=f"v_codes{e}", align_bytes=64)
            scales = keep.tile([P, P], U8, name=f"v_scales{e}", align_bytes=64)
            nc.vector.quantize_mx(out=codes[:].bitcast(FP8X4), scales=scales[:], in_=grouped[:].rearrange("p e a -> p (e a)"))
            v_codes.append(codes)
            v_scales.append(scales)

        pick_values(0)

        gate = keep.tile([P, 2, DV], F32, name="gate")
        nc.scalar.activation(gate[:], og_raw[:], ACT.Tanh, scale=0.5)
        factor = keep.tile([P, 2, DV], F32, name="factor")

        w_codes, w_scales = [], []
        for b in range(2):
            turned = psum.tile([P, PACK, P], F32, tag="s", name=f"p_turned{b}")
            for a in range(PACK):
                nc.tensor.transpose(turned[:, a, :], probs[b][:, a, :], ident[:])
            w_bf = keep.tile([P, P, PACK], BF16, name=f"w_bf{b}", align_bytes=64)
            nc.vector.tensor_tensor(
                w_bf[:],
                turned[:].rearrange("p a q -> p q a"),
                vs_cols[:].unsqueeze(1).to_broadcast([P, P, PACK]),
                ALU.mult,
            )
            codes = keep.tile([P, P], U32, name=f"w_codes{b}", align_bytes=64)
            scales = keep.tile([P, P], U8, name=f"w_scales{b}", align_bytes=64)
            nc.vector.quantize_mx(out=codes[:].bitcast(FP8X4), scales=scales[:], in_=w_bf[:].rearrange("p q a -> p (q a)"))
            w_codes.append(codes)
            w_scales.append(scales)

        pick_values(1)

        for b in range(2):
            nc.scalar.activation(
                factor[:, b, :], gate[:, b, :], ACT.Identity, scale=inv[:, b : b + 1], bias=inv[:, b : b + 1]
            )

        out_rows = out.rearrange("o (b p) e -> p (o b) e", p=P)
        for e in range(2):
            y = psum.tile([P, 2, P], F32, tag="y", name=f"y{e}")
            for b in range(2):
                nc.tensor.matmul_mx(
                    out=y[:, b, :],
                    lhsT=w_codes[b][:].bitcast(FP8X4),
                    lhsT_scale=w_scales[b][:],
                    rhs=v_codes[e][:].bitcast(FP8X4),
                    rhs_scale=v_scales[e][:],
                    start=True,
                    stop=True,
                )
            result = keep.tile([P, 2, P], F32, name=f"result{e}")
            nc.vector.scalar_tensor_tensor(result[:], y[:], 0.5, factor[:, :, e * P : (e + 1) * P], ALU.mult, ALU.mult)
            nc.sync.dma_start(out=out_rows[:, :, e * P : (e + 1) * P], in_=result[:])
